import numpy as np
import ml_dtypes


def mxq(x, axis, fmt="e4m3"):
    dtype, down = {"e4m3": (ml_dtypes.float8_e4m3fn, 7), "e5m2": (ml_dtypes.float8_e5m2, 14)}[fmt]
    v = np.moveaxis(np.asarray(x, np.float32).astype(ml_dtypes.bfloat16).astype(np.float64), axis, -1)
    blocks = v.reshape(v.shape[:-1] + (-1, 32))
    amax = np.abs(blocks).max(-1, keepdims=True)
    byte = np.maximum(np.where(amax > 0, np.frexp(amax)[1] - 1 + 127, 0) - down, 1)
    scale = np.exp2(byte - 127.0)
    codes = (blocks / scale).astype(np.float32).astype(dtype).astype(np.float64)
    return np.moveaxis((codes * scale).reshape(v.shape), -1, axis)


WIDE = False


def mx_kscale(k):
    if not WIDE:
        return np.ones(k)
    levels = np.array([10, -10, 5, -5, 0])
    if k % 512:
        return np.exp2(np.random.permutation(np.resize(levels, k // 32))).repeat(32)
    a = np.empty((k // 512, 16))
    for p in range(k // 512):
        a[p, :8] = np.random.permutation(np.resize(levels, 8))
        for g in range(8):
            far = levels[np.abs(levels - a[p, g]) >= 10]
            a[p, g + 8] = far[np.random.randint(len(far))]
    return np.exp2(a.ravel()).repeat(32)


def f64(x):
    return np.asarray(x).astype(np.float64)


def striped8(idx):
    return np.asarray(idx).reshape(8, -1, 16).transpose(0, 2, 1).reshape(128, -1).astype(np.uint16)


def unstriped8(offs):
    return offs.reshape(8, 16, -1).transpose(0, 2, 1).reshape(8, -1).astype(np.int64)


def pick8(x, idx, run):
    r = np.arange(len(x))
    return x[r[:, None], idx[r % (8 * run) // run]]


E2M1 = np.array([0.0, 0.5, 1.0, 1.5, 2.0, 3.0, 4.0, 6.0, -0.0, -0.5, -1.0, -1.5, -2.0, -3.0, -4.0, -6.0])


def pack_weight(w, fmt):
    k, n = w.shape
    w = f64(np.asarray(w, np.float32).astype(ml_dtypes.bfloat16)).reshape(k // 32, 32, n)
    amax = np.abs(w).max(1)
    if fmt == "e4m3":
        byte = np.frexp(amax)[1] - 1 + 127 - 7
    else:
        mant, ex = np.frexp(amax / 6.0)
        byte = np.where(mant > 0.5, ex, ex - 1) + 127
    byte = np.clip(np.where(amax > 0, byte, 1), 1, 254)
    scaled = (w * np.exp2(127.0 - byte)[:, None, :]).reshape(k, n).astype(np.float32)
    by_word = np.ascontiguousarray(scaled.reshape(k // 512, 128, 4, n).transpose(0, 1, 3, 2))
    if fmt == "e4m3":
        words = by_word.astype(ml_dtypes.float8_e4m3fn).view(np.uint8)
    else:
        c = by_word.astype(ml_dtypes.float4_e2m1fn).view(np.uint8) & 0xF
        words = (c[..., 0::2] | (c[..., 1::2] << 4)).reshape(k // 512, 128, 2 * n)
    return np.ascontiguousarray(words), np.ascontiguousarray(byte.astype(np.uint8).reshape(k // 512, 16, n))


def unpack_weight(words, scales, fmt):
    g, _, n = scales.shape
    words = np.ascontiguousarray(words).reshape(g, 128, n, -1)
    if fmt == "e4m3":
        vals = words.view(ml_dtypes.float8_e4m3fn).astype(np.float64)
    else:
        nib = np.empty((g, 128, n, 4), np.uint8)
        nib[..., 0::2] = words & 0xF
        nib[..., 1::2] = words >> 4
        vals = E2M1[nib]
    vals = vals * np.repeat(np.exp2(scales.astype(np.float64) - 127.0), 8, axis=1)[..., None]
    return vals.transpose(0, 1, 3, 2).reshape(g * 512, n)


D, V, Q, I = 512, 2048, 128, 512


def setup_inputs():
    n = np.random.standard_normal
    idx = np.stack([np.random.permutation(V)[:I] for _ in range(8)])
    fd = mx_kscale(D)
    vocp = pack_weight(n((D, V)) / fd[:, None], "e2m1")
    return {
        "hid": (n((D, Q)) * 1.0 / np.sqrt(D) * fd[:, None]).astype(np.float32),
        "voc_words": vocp[0],
        "voc_scales": vocp[1],
        "aim": (np.random.uniform(0.1, 0.6, (Q, 1))).astype(np.float32),
        "cw1": (np.random.uniform(0.5, 1.5, (1, I))).astype(np.float32),
        "sw": (np.random.uniform(20.0, 80.0, (1, I))).astype(np.float32),
        "old": (0.5 * n((Q, V))).astype(np.float32),
        "offs": striped8(idx),
    }


def reference(hid, voc_words, voc_scales, aim, cw1, sw, old, offs):
    idx = unstriped8(offs)
    vocu = unpack_weight(voc_words, voc_scales, "e2m1")
    hidq = mxq(f64(hid), 0, "e4m3")
    a = hidq.T @ vocu
    m1 = np.max(a, axis=1, keepdims=True)
    p = np.exp(a - m1)
    z = np.sum(p, axis=1, keepdims=True)
    px = np.exp(pick8(a, idx, 16) - m1)
    pm = np.sum(px * f64(cw1), axis=1, keepdims=True)
    u1 = px / pm
    du1 = f64(sw) * u1 * 2.0
    dpm = 4.0 * (pm / z - f64(aim)) * 2.0 / z + np.sum(du1 * px / np.square(pm) * (-1.0), axis=1, keepdims=True)
    dpx = du1 / pm + dpm * f64(cw1)
    dz = 4.0 * (pm / z - f64(aim)) * 2.0 * pm / np.square(z) * (-1.0)
    e1 = dpx * px
    s1 = np.zeros((Q, V))
    s1[np.arange(Q)[:, None], idx[np.arange(Q) % 128 // 16]] = e1
    da = dz * p + s1
    y = da * 256.0 + f64(old)
    return y

@@ -1,0 +1,186 @@
+from contextlib import ExitStack
+
+import concourse.mybir as mybir
+from concourse.masks import make_identity
+
+D, V, Q, I = 512, 2048, 128, 512
+FLOPS = 2 * D * V * Q
+
+F32 = mybir.dt.float32
+BF16 = mybir.dt.bfloat16
+I32 = mybir.dt.int32
+U32 = mybir.dt.uint32
+U16 = mybir.dt.uint16
+U8 = mybir.dt.uint8
+FP8X4 = mybir.dt.float8_e4m3fn_x4
+FP4X4 = mybir.dt.float4_e2m1fn_x4
+ALU = mybir.AluOpType
+ACT = mybir.ActivationFunctionType
+
+P = 128
+PACK = 4
+N = 512
+CHUNKS = V // N
+
+
+def tile_attend_bcoverage_heads_kernel(tc, hid, voc_words, voc_scales, aim, cw1, sw, old, offs, out):
+    nc = tc.nc
+    with ExitStack() as ctx:
+        keep = ctx.enter_context(tc.tile_pool(name="keep", bufs=1))
+        psum = ctx.enter_context(tc.psum_pool(name="psum", bufs=1))
+
+        offsets = keep.tile([P, I // 16], U16, name="offsets")
+        hid_raw = keep.tile([P, PACK, Q], F32, name="hid_raw")
+        words = [keep.tile([P, V], U8, name=f"words{h}", align_bytes=64) for h in range(2)]
+        voc_plane = keep.tile([P, V], U8, name="voc_plane", align_bytes=64)
+        cw_rows = keep.tile([P, PACK], F32, name="cw_rows")
+        sw_rows = keep.tile([P, PACK], F32, name="sw_rows")
+        aim_col = keep.tile([P, 1], F32, name="aim_col")
+        old_sb = keep.tile([P, V], F32, name="old_sb")
+        s1 = keep.tile([P, V], F32, name="s1")
+        ident = keep.tile([P, P], F32, name="ident")
+        warm = keep.tile([P, 1], F32, name="warm")
+
+        nc.sync.dma_start(out=hid_raw[:], in_=hid.rearrange("(p t) q -> p t q", t=PACK))
+        nc.vector.memset(voc_plane[:].bitcast(U32), 0)
+        for r in range(4):
+            nc.scalar.dma_start(
+                out=voc_plane[r:P:32, :].bitcast(I32), in_=voc_scales[0, r:16:4, :].bitcast(I32)
+            )
+        for h in range(2):
+            nc.sync.dma_start(
+                out=words[h][:].bitcast(I32), in_=voc_words[0, :, h * V : (h + 1) * V].bitcast(I32)
+            )
+        nc.sync.dma_start(offsets[:], offs)
+        nc.sync.dma_start(out=cw_rows[:], in_=cw1.rearrange("o (p c) -> (o p) c", c=PACK))
+        nc.sync.dma_start(out=sw_rows[:], in_=sw.rearrange("o (p c) -> (o p) c", c=PACK))
+        nc.sync.dma_start(out=aim_col[:], in_=aim)
+        for h in range(2):
+            cols = slice(h * V // 2, (h + 1) * V // 2)
+            nc.sync.dma_start(out=old_sb[:, cols], in_=old[:, cols])
+
+        nc.vector.memset(warm[:], 0.0)
+        nc.scalar.activation(out=warm[:], in_=warm[:], func=ACT.Exp)
+        nc.vector.memset(s1[:], 0.0)
+        make_identity(nc, ident[:])
+
+        grouped = keep.tile([P, Q, PACK], BF16, name="grouped", align_bytes=64)
+        nc.vector.tensor_copy(
+            out=grouped[:].rearrange("p (c i) t -> p c t i", i=4),
+            in_=hid_raw[:].rearrange("p t (c i) -> p c t i", i=4),
+        )
+        hid_codes = keep.tile([P, Q], U32, name="hid_codes", align_bytes=64)
+        hid_plane = keep.tile([P, Q], U8, name="hid_plane", align_bytes=64)
+        nc.vector.quantize_mx(
+            out=hid_codes[:].bitcast(FP8X4), scales=hid_plane[:], in_=grouped[:].rearrange("p q t -> p (q t)")
+        )
+
+        a_sb = keep.tile([P, V], F32, name="a_sb")
+        p_sb = keep.tile([P, V], F32, name="p_sb")
+        mx = keep.tile([P, CHUNKS], F32, name="mx")
+        zs = keep.tile([P, CHUNKS], F32, name="zs")
+        ns = keep.tile([P, CHUNKS], F32, name="ns")
+        rise = keep.tile([P, 1], F32, name="rise")
+        ax = keep.tile([P, I], F32, name="ax")
+        px = keep.tile([P, I], F32, name="px")
+        for j in range(CHUNKS):
+            cols = slice(j * N, (j + 1) * N)
+            bank = psum.tile([P, N], F32, name=f"bank{j}", tag=f"bank{j}")
+            nc.tensor.matmul_mx(
+                out=bank[:],
+                lhsT=hid_codes[:].bitcast(FP8X4),
+                lhsT_scale=hid_plane[:],
+                rhs=words[j // 2][:, (j % 2) * 2 * N : (j % 2 + 1) * 2 * N].bitcast(FP4X4),
+                rhs_scale=voc_plane[:, cols],
+                start=True,
+                stop=True,
+            )
+            nc.vector.tensor_scalar(
+                out=a_sb[:, cols], in0=bank[:], scalar1=1.0, scalar2=None, op0=ALU.mult, op1=ALU.max,
+                accum_out=mx[:, j : j + 1],
+            )
+            if j == 0:
+                nc.gpsimd.tensor_scalar(
+                    out=ns[:, 0:1], in0=mx[:, 0:1], scalar1=-1.0, scalar2=0.0, op0=ALU.mult, op1=ALU.add
+                )
+            elif j < CHUNKS - 1:
+                nc.gpsimd.tensor_scalar(
+                    out=ns[:, j : j + 1], in0=mx[:, j : j + 1], scalar1=-1.0, scalar2=ns[:, j - 1 : j],
+                    op0=ALU.mult, op1=ALU.min,
+                )
+
+        def exp_chunk(j):
+            cols = slice(j * N, (j + 1) * N)
+            nc.scalar.activation(
+                out=p_sb[:, cols], in_=a_sb[:, cols], func=ACT.Exp, bias=ns[:, j : j + 1], accum_out=zs[:, j : j + 1]
+            )
+
+        for j in range(CHUNKS - 1):
+            exp_chunk(j)
+        nc.vector.tensor_copy(out=ax[:], in_=a_sb[:].indirect(offsets[:]))
+        last = CHUNKS - 1
+        nm = ns[:, last:]
+        nc.scalar.activation(out=rise[:], in_=mx[:, last:], func=ACT.Relu, bias=ns[:, last - 1 : last])
+        nc.scalar.activation(out=nm, in_=rise[:], func=ACT.Identity, scale=-1.0, bias=ns[:, last - 1 : last])
+        exp_chunk(last)
+        f = keep.tile([P, CHUNKS], F32, name="f")
+        nc.scalar.activation(out=f[:], in_=ns[:], func=ACT.Exp, scale=-1.0, bias=nm)
+        nc.scalar.activation(out=px[:], in_=ax[:], func=ACT.Exp, bias=nm)
+        sq = keep.tile([P, I], F32, name="sq")
+        nc.scalar.activation(out=sq[:], in_=px[:], func=ACT.Square)
+
+        def spread(rows, tag):
+            bank = psum.tile([P, PACK, P], F32, name="spread_" + tag, tag=tag)
+            for c in range(PACK):
+                nc.tensor.transpose(bank[:, c, :], rows[:, c : c + 1].to_broadcast([P, P]), ident[:])
+            return bank[:].rearrange("p c n -> p n c")
+
+        cw_all = spread(cw_rows, "bank0")
+        sw_all = spread(sw_rows, "bank1")
+
+        def by4(t):
+            return t[:].rearrange("p (n c) -> p n c", c=PACK)
+
+        def col(name):
+            return keep.tile([P, 1], F32, name=name)
+
+        w = keep.tile([P, I], F32, name="w")
+        x = keep.tile([P, I], F32, name="x")
+        y = keep.tile([P, I], F32, name="y")
+        pm, z, rpm, rz, big_a, k, k2, acc, nb, nr = [
+            col(n) for n in ("pm", "z", "rpm", "rz", "big_a", "k", "k2", "acc", "nb", "nr")
+        ]
+        fz = keep.tile([P, CHUNKS], F32, name="fz")
+        cj = keep.tile([P, CHUNKS], F32, name="cj")
+        nc.vector.scalar_tensor_tensor(
+            out=fz[:], in0=f[:], scalar=1.0, in1=zs[:], op0=ALU.mult, op1=ALU.mult, accum_out=z[:]
+        )
+        nc.vector.reciprocal(out=rz[:], in_=z[:])
+        nc.vector.scalar_tensor_tensor(
+            out=by4(w), in0=by4(px), scalar=1.0, in1=cw_all, op0=ALU.mult, op1=ALU.mult, accum_out=pm[:]
+        )
+        nc.vector.reciprocal(out=rpm[:], in_=pm[:])
+        nc.vector.tensor_scalar(out=big_a[:], in0=rpm[:], scalar1=rpm[:], scalar2=512.0, op0=ALU.mult, op1=ALU.mult)
+        nc.vector.tensor_scalar(out=k[:], in0=rz[:], scalar1=pm[:], scalar2=aim_col[:], op0=ALU.mult, op1=ALU.subtract)
+        nc.vector.tensor_scalar(out=nr[:], in0=rz[:], scalar1=pm[:], scalar2=-1.0, op0=ALU.mult, op1=ALU.mult)
+        nc.vector.scalar_tensor_tensor(
+            out=by4(x), in0=by4(sq), scalar=big_a[:], in1=sw_all, op0=ALU.mult, op1=ALU.mult, accum_out=acc[:]
+        )
+        nc.vector.tensor_scalar(out=k2[:], in0=k[:], scalar1=rz[:], scalar2=2048.0, op0=ALU.mult, op1=ALU.mult)
+        nc.vector.tensor_scalar(out=nb[:], in0=acc[:], scalar1=rpm[:], scalar2=k2[:], op0=ALU.mult, op1=ALU.subtract)
+        nc.vector.tensor_scalar(out=cj[:], in0=f[:], scalar1=k2[:], scalar2=nr[:], op0=ALU.mult, op1=ALU.mult)
+        nc.vector.tensor_scalar(out=y[:], in0=w[:], scalar1=nb[:], scalar2=-1.0, op0=ALU.mult, op1=ALU.mult)
+        nc.vector.tensor_tensor(out=s1[:].indirect(offsets[:]), in0=x[:], in1=y[:], op=ALU.add)
+
+        base = keep.tile([P, V], F32, name="base")
+        res = keep.tile([P, V], F32, name="res")
+        for j in range(CHUNKS):
+            cols = slice(j * N, (j + 1) * N)
+            nc.vector.scalar_tensor_tensor(
+                out=base[:, cols], in0=p_sb[:, cols], scalar=cj[:, j : j + 1], in1=old_sb[:, cols],
+                op0=ALU.mult, op1=ALU.add,
+            )
+        for j in range(CHUNKS):
+            cols = slice(j * N, (j + 1) * N)
+            nc.vector.tensor_tensor(out=res[:, cols], in0=base[:, cols], in1=s1[:, cols], op=ALU.add)
+            nc.sync.dma_start(out=out[:, cols], in_=res[:, cols])

@@ -31,7 +31,9 @@ def tile_attend_bcoverage_heads_kernel(tc, hid, voc_words, voc_scales, aim, cw1,
 
         offsets = keep.tile([P, I // 16], U16, name="offsets")
         hid_raw = keep.tile([P, PACK, Q], F32, name="hid_raw")
-        words = [keep.tile([P, V], U8, name=f"words{h}", align_bytes=64) for h in range(2)]
+        spans = ((0, 1), (1, 2), (2, 4))
+        word_tiles = [keep.tile([P, (b - a) * 2 * N], U8, name=f"words{a}", align_bytes=64) for a, b in spans]
+        words = [t[:, (j - a) * 2 * N : (j - a + 1) * 2 * N] for t, (a, b) in zip(word_tiles, spans) for j in range(a, b)]
         voc_plane = keep.tile([P, V], U8, name="voc_plane", align_bytes=64)
         cw_rows = keep.tile([P, PACK], F32, name="cw_rows")
         sw_rows = keep.tile([P, PACK], F32, name="sw_rows")
@@ -42,15 +44,13 @@ def tile_attend_bcoverage_heads_kernel(tc, hid, voc_words, voc_scales, aim, cw1,
         warm = keep.tile([P, 1], F32, name="warm")
 
         nc.sync.dma_start(out=hid_raw[:], in_=hid.rearrange("(p t) q -> p t q", t=PACK))
-        nc.vector.memset(voc_plane[:].bitcast(U32), 0)
+        nc.gpsimd.memset(voc_plane[:].bitcast(U32), 0)
         for r in range(4):
-            nc.scalar.dma_start(
+            nc.sync.dma_start(
                 out=voc_plane[r:P:32, :].bitcast(I32), in_=voc_scales[0, r:16:4, :].bitcast(I32)
             )
-        for h in range(2):
-            nc.sync.dma_start(
-                out=words[h][:].bitcast(I32), in_=voc_words[0, :, h * V : (h + 1) * V].bitcast(I32)
-            )
+        for t, (a, b) in zip(word_tiles, spans):
+            nc.sync.dma_start(out=t[:].bitcast(I32), in_=voc_words[0, :, a * 2 * N : b * 2 * N].bitcast(I32))
         nc.sync.dma_start(offsets[:], offs)
         nc.sync.dma_start(out=cw_rows[:], in_=cw1.rearrange("o (p c) -> (o p) c", c=PACK))
         nc.sync.dma_start(out=sw_rows[:], in_=sw.rearrange("o (p c) -> (o p) c", c=PACK))
@@ -65,23 +65,29 @@ def tile_attend_bcoverage_heads_kernel(tc, hid, voc_words, voc_scales, aim, cw1,
         make_identity(nc, ident[:])
 
         grouped = keep.tile([P, Q, PACK], BF16, name="grouped", align_bytes=64)
-        nc.vector.tensor_copy(
-            out=grouped[:].rearrange("p (c i) t -> p c t i", i=4),
-            in_=hid_raw[:].rearrange("p t (c i) -> p c t i", i=4),
-        )
         hid_codes = keep.tile([P, Q], U32, name="hid_codes", align_bytes=64)
         hid_plane = keep.tile([P, Q], U8, name="hid_plane", align_bytes=64)
-        nc.vector.quantize_mx(
-            out=hid_codes[:].bitcast(FP8X4), scales=hid_plane[:], in_=grouped[:].rearrange("p q t -> p (q t)")
-        )
+        halves = (slice(0, Q // 2), slice(Q // 2, Q))
+        for qs in halves:
+            nc.vector.tensor_copy(
+                out=grouped[:, qs, :].rearrange("p (c i) t -> p c t i", i=4),
+                in_=hid_raw[:, :, qs].rearrange("p t (c i) -> p c t i", i=4),
+            )
+        for qs in halves:
+            nc.vector.quantize_mx(
+                out=hid_codes[:, qs].bitcast(FP8X4), scales=hid_plane[:, qs],
+                in_=grouped[:, qs, :].rearrange("p q t -> p (q t)"),
+            )
 
         a_sb = keep.tile([P, V], F32, name="a_sb")
         p_sb = keep.tile([P, V], F32, name="p_sb")
-        mx = keep.tile([P, CHUNKS], F32, name="mx")
         zs = keep.tile([P, CHUNKS], F32, name="zs")
-        ns = keep.tile([P, CHUNKS], F32, name="ns")
-        rise = keep.tile([P, 1], F32, name="rise")
+        ns = keep.tile([P, CHUNKS - 1], F32, name="ns")
+        nm = keep.tile([P, 1], F32, name="nm")
+        f = keep.tile([P, CHUNKS], F32, name="f")
+        nc.vector.memset(f[:, CHUNKS - 1 :], 1.0)
         ax = keep.tile([P, I], F32, name="ax")
+        mx = ax[:, :CHUNKS]
         px = keep.tile([P, I], F32, name="px")
         for j in range(CHUNKS):
             cols = slice(j * N, (j + 1) * N)
@@ -90,7 +96,7 @@ def tile_attend_bcoverage_heads_kernel(tc, hid, voc_words, voc_scales, aim, cw1,
                 out=bank[:],
                 lhsT=hid_codes[:].bitcast(FP8X4),
                 lhsT_scale=hid_plane[:],
-                rhs=words[j // 2][:, (j % 2) * 2 * N : (j % 2 + 1) * 2 * N].bitcast(FP4X4),
+                rhs=words[j].bitcast(FP4X4),
                 rhs_scale=voc_plane[:, cols],
                 start=True,
                 stop=True,
@@ -111,23 +117,23 @@ def tile_attend_bcoverage_heads_kernel(tc, hid, voc_words, voc_scales, aim, cw1,
 
         def exp_chunk(j):
             cols = slice(j * N, (j + 1) * N)
+            shift = ns[:, j : j + 1] if j < CHUNKS - 1 else nm[:]
             nc.scalar.activation(
-                out=p_sb[:, cols], in_=a_sb[:, cols], func=ACT.Exp, bias=ns[:, j : j + 1], accum_out=zs[:, j : j + 1]
+                out=p_sb[:, cols], in_=a_sb[:, cols], func=ACT.Exp, bias=shift, accum_out=zs[:, j : j + 1]
             )
 
         for j in range(CHUNKS - 1):
             exp_chunk(j)
-        nc.vector.tensor_copy(out=ax[:], in_=a_sb[:].indirect(offsets[:]))
         last = CHUNKS - 1
-        nm = ns[:, last:]
-        nc.scalar.activation(out=rise[:], in_=mx[:, last:], func=ACT.Relu, bias=ns[:, last - 1 : last])
-        nc.scalar.activation(out=nm, in_=rise[:], func=ACT.Identity, scale=-1.0, bias=ns[:, last - 1 : last])
+        nc.vector.tensor_scalar(
+            out=nm[:], in0=mx[:, last:], scalar1=-1.0, scalar2=ns[:, last - 1 :], op0=ALU.mult, op1=ALU.min
+        )
+        nc.vector.tensor_copy(out=ax[:], in_=a_sb[:].indirect(offsets[:]))
         exp_chunk(last)
-        f = keep.tile([P, CHUNKS], F32, name="f")
-        nc.scalar.activation(out=f[:], in_=ns[:], func=ACT.Exp, scale=-1.0, bias=nm)
-        nc.scalar.activation(out=px[:], in_=ax[:], func=ACT.Exp, bias=nm)
-        sq = keep.tile([P, I], F32, name="sq")
-        nc.scalar.activation(out=sq[:], in_=px[:], func=ACT.Square)
+        nc.scalar.activation(out=f[:, :last], in_=ns[:], func=ACT.Exp, scale=-1.0, bias=nm[:])
+        nc.scalar.activation(out=px[:], in_=ax[:], func=ACT.Exp, bias=nm[:])
+        sq = keep.tile([P, I + 1 + CHUNKS], F32, name="sq")
+        nc.scalar.activation(out=sq[:, :I], in_=px[:], func=ACT.Square)
 
         def spread(rows, tag):
             bank = psum.tile([P, PACK, P], F32, name="spread_" + tag, tag=tag)
@@ -135,8 +141,8 @@ def tile_attend_bcoverage_heads_kernel(tc, hid, voc_words, voc_scales, aim, cw1,
                 nc.tensor.transpose(bank[:, c, :], rows[:, c : c + 1].to_broadcast([P, P]), ident[:])
             return bank[:].rearrange("p c n -> p n c")
 
-        cw_all = spread(cw_rows, "bank0")
-        sw_all = spread(sw_rows, "bank1")
+        cw_all = spread(cw_rows, "cw")
+        sw_all = spread(sw_rows, "sw")
 
         def by4(t):
             return t[:].rearrange("p (n c) -> p n c", c=PACK)
@@ -145,42 +151,91 @@ def tile_attend_bcoverage_heads_kernel(tc, hid, voc_words, voc_scales, aim, cw1,
             return keep.tile([P, 1], F32, name=name)
 
         w = keep.tile([P, I], F32, name="w")
-        x = keep.tile([P, I], F32, name="x")
+        x = keep.tile([P, I + 1], F32, name="x")
         y = keep.tile([P, I], F32, name="y")
-        pm, z, rpm, rz, big_a, k, k2, acc, nb, nr = [
-            col(n) for n in ("pm", "z", "rpm", "rz", "big_a", "k", "k2", "acc", "nb", "nr")
-        ]
+        sw_sb = keep.tile([P, I + 1], F32, name="sw_sb")
+        pm = sw_sb[:, I:]
+        z, rpm, rz, big_a, acc, nrpm = [col(n) for n in ("z", "rpm", "rz", "big_a", "acc", "nrpm")]
         fz = keep.tile([P, CHUNKS], F32, name="fz")
-        cj = keep.tile([P, CHUNKS], F32, name="cj")
+        factors = keep.tile([P, 2], F32, name="factors")
+        aims = keep.tile([P, 2], F32, name="aims")
+        rzs = keep.tile([P, 2], F32, name="rzs")
+        terms = keep.tile([P, CHUNKS + 2], F32, name="terms")
+        nc.vector.memset(factors[:, 0:1], -2048.0)
+        nc.vector.memset(factors[:, 1:2], 1.0 / 512.0)
+        nc.vector.memset(aims[:, 1:2], 0.0)
+        nc.vector.tensor_scalar(out=aims[:, 0:1], in0=aim_col[:], scalar1=2048.0, scalar2=None, op0=ALU.mult)
+        nc.vector.tensor_copy(out=sw_sb[:, :I].rearrange("p (n c) -> p n c", c=PACK), in_=sw_all)
         nc.vector.scalar_tensor_tensor(
             out=fz[:], in0=f[:], scalar=1.0, in1=zs[:], op0=ALU.mult, op1=ALU.mult, accum_out=z[:]
         )
         nc.vector.reciprocal(out=rz[:], in_=z[:])
-        nc.vector.scalar_tensor_tensor(
-            out=by4(w), in0=by4(px), scalar=1.0, in1=cw_all, op0=ALU.mult, op1=ALU.mult, accum_out=pm[:]
+        nc.vector.tensor_scalar(out=rzs[:], in0=factors[:], scalar1=rz[:], scalar2=None, op0=ALU.mult)
+        nc.vector.tensor_scalar(
+            out=terms[:, 2:], in0=f[:], scalar1=rz[:], scalar2=rz[:], op0=ALU.mult, op1=ALU.mult
         )
-        nc.vector.reciprocal(out=rpm[:], in_=pm[:])
+        nc.vector.scalar_tensor_tensor(
+            out=by4(w), in0=by4(px), scalar=1.0, in1=cw_all, op0=ALU.mult, op1=ALU.mult, accum_out=pm
+        )
+        nc.vector.reciprocal(out=rpm[:], in_=pm)
+        nc.vector.scalar_tensor_tensor(
+            out=terms[:, :2], in0=rzs[:], scalar=pm, in1=aims[:], op0=ALU.mult, op1=ALU.add
+        )
         nc.vector.tensor_scalar(out=big_a[:], in0=rpm[:], scalar1=rpm[:], scalar2=512.0, op0=ALU.mult, op1=ALU.mult)
-        nc.vector.tensor_scalar(out=k[:], in0=rz[:], scalar1=pm[:], scalar2=aim_col[:], op0=ALU.mult, op1=ALU.subtract)
-        nc.vector.tensor_scalar(out=nr[:], in0=rz[:], scalar1=pm[:], scalar2=-1.0, op0=ALU.mult, op1=ALU.mult)
-        nc.vector.scalar_tensor_tensor(
-            out=by4(x), in0=by4(sq), scalar=big_a[:], in1=sw_all, op0=ALU.mult, op1=ALU.mult, accum_out=acc[:]
+        nc.vector.tensor_scalar(
+            out=sq[:, I:], in0=terms[:, 1:], scalar1=terms[:, 0:1], scalar2=pm, op0=ALU.mult, op1=ALU.mult
         )
-        nc.vector.tensor_scalar(out=k2[:], in0=k[:], scalar1=rz[:], scalar2=2048.0, op0=ALU.mult, op1=ALU.mult)
-        nc.vector.tensor_scalar(out=nb[:], in0=acc[:], scalar1=rpm[:], scalar2=k2[:], op0=ALU.mult, op1=ALU.subtract)
-        nc.vector.tensor_scalar(out=cj[:], in0=f[:], scalar1=k2[:], scalar2=nr[:], op0=ALU.mult, op1=ALU.mult)
-        nc.vector.tensor_scalar(out=y[:], in0=w[:], scalar1=nb[:], scalar2=-1.0, op0=ALU.mult, op1=ALU.mult)
-        nc.vector.tensor_tensor(out=s1[:].indirect(offsets[:]), in0=x[:], in1=y[:], op=ALU.add)
+        cj = sq[:, I + 1 :]
+        nc.vector.tensor_scalar(out=nrpm[:], in0=rpm[:], scalar1=-1.0, scalar2=None, op0=ALU.mult)
+        nc.vector.scalar_tensor_tensor(
+            out=x[:], in0=sq[:, : I + 1], scalar=big_a[:], in1=sw_sb[:], op0=ALU.mult, op1=ALU.mult, accum_out=acc[:]
+        )
+        nc.vector.tensor_scalar(out=y[:], in0=w[:], scalar1=acc[:], scalar2=nrpm[:], op0=ALU.mult, op1=ALU.mult)
+        nc.vector.tensor_tensor(out=s1[:].indirect(offsets[:]), in0=x[:, :I], in1=y[:], op=ALU.add)
 
-        base = keep.tile([P, V], F32, name="base")
+        cp = keep.tile([P, V], F32, name="cp")
+        turned = keep.tile([P, V], F32, name="turned")
         res = keep.tile([P, V], F32, name="res")
+        blocks = N // P
+
+        def block(t, j, b):
+            return t[:, j * N + b * P : j * N + (b + 1) * P]
+
+        sums = []
         for j in range(CHUNKS):
+            bank = psum.tile([P, N], F32, name=f"sum{j}", tag=f"bank{j}")
+            for b in range(blocks):
+                nc.tensor.matmul(
+                    out=block(bank, 0, b), lhsT=block(old_sb, j, b), rhs=ident[:], is_transpose=True,
+                    start=(b == 0), stop=False,
+                )
+            sums.append(bank)
+
+        def scale_and_add(j):
             cols = slice(j * N, (j + 1) * N)
-            nc.vector.scalar_tensor_tensor(
-                out=base[:, cols], in0=p_sb[:, cols], scalar=cj[:, j : j + 1], in1=old_sb[:, cols],
-                op0=ALU.mult, op1=ALU.add,
-            )
-        for j in range(CHUNKS):
+            nc.scalar.activation(out=cp[:, cols], in_=p_sb[:, cols], func=ACT.Copy, scale=cj[:, j : j + 1])
+            for b in range(blocks):
+                nc.tensor.matmul(
+                    out=block(sums[j], 0, b), lhsT=block(cp, j, b), rhs=ident[:], is_transpose=True,
+                    start=False, stop=(b == blocks - 1),
+                )
+
+        backs = []
+
+        def turn_back(j):
             cols = slice(j * N, (j + 1) * N)
-            nc.vector.tensor_tensor(out=res[:, cols], in0=base[:, cols], in1=s1[:, cols], op=ALU.add)
+            nc.scalar.copy(out=turned[:, cols], in_=sums[j][:])
+            bank = psum.tile([P, N], F32, name=f"back{j}", tag=("back0", "back1", "sw", "cw")[j])
+            for b in range(blocks):
+                nc.tensor.transpose(block(bank, 0, b), block(turned, j, b), ident[:])
+            backs.append(bank)
+
+        scale_and_add(0)
+        for j in range(1, CHUNKS):
+            scale_and_add(j)
+            turn_back(j - 1)
+        turn_back(last)
+        for j, a, b in ((0, 0, 256), (0, 256, 512), (1, 0, 512), (2, 0, 512), (3, 0, 256), (3, 256, 384), (3, 384, 512)):
+            cols = slice(j * N + a, j * N + b)
+            nc.vector.tensor_tensor(out=res[:, cols], in0=backs[j][:, a:b], in1=s1[:, cols], op=ALU.add)
             nc.sync.dma_start(out=out[:, cols], in_=res[:, cols])

@@ -44,7 +44,6 @@ def tile_attend_bcoverage_heads_kernel(tc, hid, voc_words, voc_scales, aim, cw1,
         warm = keep.tile([P, 1], F32, name="warm")
 
         nc.sync.dma_start(out=hid_raw[:], in_=hid.rearrange("(p t) q -> p t q", t=PACK))
-        nc.gpsimd.memset(voc_plane[:].bitcast(U32), 0)
         for r in range(4):
             nc.sync.dma_start(
                 out=voc_plane[r:P:32, :].bitcast(I32), in_=voc_scales[0, r:16:4, :].bitcast(I32)
@@ -68,8 +67,8 @@ def tile_attend_bcoverage_heads_kernel(tc, hid, voc_words, voc_scales, aim, cw1,
         hid_codes = keep.tile([P, Q], U32, name="hid_codes", align_bytes=64)
         hid_plane = keep.tile([P, Q], U8, name="hid_plane", align_bytes=64)
         halves = (slice(0, Q // 2), slice(Q // 2, Q))
-        for qs in halves:
-            nc.vector.tensor_copy(
+        for qs, copy in zip(halves, (nc.vector.tensor_copy, nc.scalar.copy)):
+            copy(
                 out=grouped[:, qs, :].rearrange("p (c i) t -> p c t i", i=4),
                 in_=hid_raw[:, :, qs].rearrange("p t (c i) -> p c t i", i=4),
             )
@@ -87,7 +86,7 @@ def tile_attend_bcoverage_heads_kernel(tc, hid, voc_words, voc_scales, aim, cw1,
         f = keep.tile([P, CHUNKS], F32, name="f")
         nc.vector.memset(f[:, CHUNKS - 1 :], 1.0)
         ax = keep.tile([P, I], F32, name="ax")
-        mx = ax[:, :CHUNKS]
+        mx = keep.tile([P, CHUNKS], F32, name="mx")
         px = keep.tile([P, I], F32, name="px")
         for j in range(CHUNKS):
             cols = slice(j * N, (j + 1) * N)
@@ -125,7 +124,7 @@ def tile_attend_bcoverage_heads_kernel(tc, hid, voc_words, voc_scales, aim, cw1,
         for j in range(CHUNKS - 1):
             exp_chunk(j)
         last = CHUNKS - 1
-        nc.vector.tensor_scalar(
+        nc.gpsimd.tensor_scalar(
             out=nm[:], in0=mx[:, last:], scalar1=-1.0, scalar2=ns[:, last - 1 :], op0=ALU.mult, op1=ALU.min
         )
         nc.vector.tensor_copy(out=ax[:], in_=a_sb[:].indirect(offsets[:]))
@@ -230,12 +229,11 @@ def tile_attend_bcoverage_heads_kernel(tc, hid, voc_words, voc_scales, aim, cw1,
                 nc.tensor.transpose(block(bank, 0, b), block(turned, j, b), ident[:])
             backs.append(bank)
 
-        scale_and_add(0)
-        for j in range(1, CHUNKS):
+        for j in range(CHUNKS):
             scale_and_add(j)
-            turn_back(j - 1)
-        turn_back(last)
-        for j, a, b in ((0, 0, 256), (0, 256, 512), (1, 0, 512), (2, 0, 512), (3, 0, 256), (3, 256, 384), (3, 384, 512)):
+        for j in range(CHUNKS):
+            turn_back(j)
+        for j, a, b in ((0, 0, 128), (0, 128, 512), (1, 0, 512), (2, 0, 512), (3, 0, 256), (3, 256, 384), (3, 384, 512)):
             cols = slice(j * N + a, j * N + b)
             nc.vector.tensor_tensor(out=res[:, cols], in0=backs[j][:, a:b], in1=s1[:, cols], op=ALU.add)
             nc.sync.dma_start(out=out[:, cols], in_=res[:, cols])

@@ -21,6 +21,24 @@ P = 128
 PACK = 4
 N = 512
 CHUNKS = V // N
+LAST = CHUNKS - 1
+BLOCKS = N // P
+WORD_BYTES = 2
+QUADRANT = 32
+WORD_LOADS = ((0, 1), (1, 2), (2, 4))
+PIECES = ((0, 0, 128), (0, 128, 512), (1, 0, 512), (2, 0, 512), (3, 0, 256), (3, 256, 384), (3, 384, 512))
+
+
+def chunk(j):
+    return slice(j * N, (j + 1) * N)
+
+
+def block(tile, j, b):
+    return tile[:, j * N + b * P : j * N + (b + 1) * P]
+
+
+def by_fours(ap):
+    return ap.rearrange("p (n c) -> p n c", c=PACK)
 
 
 def tile_attend_bcoverage_heads_kernel(tc, hid, voc_words, voc_scales, aim, cw1, sw, old, offs, out):
@@ -31,10 +49,15 @@ def tile_attend_bcoverage_heads_kernel(tc, hid, voc_words, voc_scales, aim, cw1,
 
         offsets = keep.tile([P, I // 16], U16, name="offsets")
         hid_raw = keep.tile([P, PACK, Q], F32, name="hid_raw")
-        spans = ((0, 1), (1, 2), (2, 4))
-        word_tiles = [keep.tile([P, (b - a) * 2 * N], U8, name=f"words{a}", align_bytes=64) for a, b in spans]
-        words = [t[:, (j - a) * 2 * N : (j - a + 1) * 2 * N] for t, (a, b) in zip(word_tiles, spans) for j in range(a, b)]
-        voc_plane = keep.tile([P, V], U8, name="voc_plane", align_bytes=64)
+        word_tiles = [
+            keep.tile([P, (b - a) * WORD_BYTES * N], U8, name=f"words{a}", align_bytes=64) for a, b in WORD_LOADS
+        ]
+        words = [
+            tile[:, (j - a) * WORD_BYTES * N : (j - a + 1) * WORD_BYTES * N]
+            for tile, (a, b) in zip(word_tiles, WORD_LOADS)
+            for j in range(a, b)
+        ]
+        voc_scale_sb = keep.tile([P, V], U8, name="voc_scale_sb", align_bytes=64)
         cw_rows = keep.tile([P, PACK], F32, name="cw_rows")
         sw_rows = keep.tile([P, PACK], F32, name="sw_rows")
         aim_col = keep.tile([P, 1], F32, name="aim_col")
@@ -46,10 +69,13 @@ def tile_attend_bcoverage_heads_kernel(tc, hid, voc_words, voc_scales, aim, cw1,
         nc.sync.dma_start(out=hid_raw[:], in_=hid.rearrange("(p t) q -> p t q", t=PACK))
         for r in range(4):
             nc.sync.dma_start(
-                out=voc_plane[r:P:32, :].bitcast(I32), in_=voc_scales[0, r:16:4, :].bitcast(I32)
+                out=voc_scale_sb[r:P:QUADRANT, :].bitcast(I32), in_=voc_scales[0, r:16:4, :].bitcast(I32)
             )
-        for t, (a, b) in zip(word_tiles, spans):
-            nc.sync.dma_start(out=t[:].bitcast(I32), in_=voc_words[0, :, a * 2 * N : b * 2 * N].bitcast(I32))
+        for tile, (a, b) in zip(word_tiles, WORD_LOADS):
+            nc.sync.dma_start(
+                out=tile[:].bitcast(I32),
+                in_=voc_words[0, :, a * WORD_BYTES * N : b * WORD_BYTES * N].bitcast(I32),
+            )
         nc.sync.dma_start(offsets[:], offs)
         nc.sync.dma_start(out=cw_rows[:], in_=cw1.rearrange("o (p c) -> (o p) c", c=PACK))
         nc.sync.dma_start(out=sw_rows[:], in_=sw.rearrange("o (p c) -> (o p) c", c=PACK))
@@ -65,7 +91,7 @@ def tile_attend_bcoverage_heads_kernel(tc, hid, voc_words, voc_scales, aim, cw1,
 
         grouped = keep.tile([P, Q, PACK], BF16, name="grouped", align_bytes=64)
         hid_codes = keep.tile([P, Q], U32, name="hid_codes", align_bytes=64)
-        hid_plane = keep.tile([P, Q], U8, name="hid_plane", align_bytes=64)
+        hid_scale_sb = keep.tile([P, Q], U8, name="hid_scale_sb", align_bytes=64)
         halves = (slice(0, Q // 2), slice(Q // 2, Q))
         for qs, copy in zip(halves, (nc.vector.tensor_copy, nc.scalar.copy)):
             copy(
@@ -74,63 +100,65 @@ def tile_attend_bcoverage_heads_kernel(tc, hid, voc_words, voc_scales, aim, cw1,
             )
         for qs in halves:
             nc.vector.quantize_mx(
-                out=hid_codes[:, qs].bitcast(FP8X4), scales=hid_plane[:, qs],
+                out=hid_codes[:, qs].bitcast(FP8X4),
+                scales=hid_scale_sb[:, qs],
                 in_=grouped[:, qs, :].rearrange("p q t -> p (q t)"),
             )
 
         a_sb = keep.tile([P, V], F32, name="a_sb")
         p_sb = keep.tile([P, V], F32, name="p_sb")
-        zs = keep.tile([P, CHUNKS], F32, name="zs")
-        ns = keep.tile([P, CHUNKS - 1], F32, name="ns")
-        nm = keep.tile([P, 1], F32, name="nm")
-        f = keep.tile([P, CHUNKS], F32, name="f")
-        nc.vector.memset(f[:, CHUNKS - 1 :], 1.0)
+        z_parts = keep.tile([P, CHUNKS], F32, name="z_parts")
+        neg_run = keep.tile([P, LAST], F32, name="neg_run")
+        neg_max = keep.tile([P, 1], F32, name="neg_max")
+        mend = keep.tile([P, CHUNKS], F32, name="mend")
+        nc.vector.memset(mend[:, LAST:], 1.0)
         ax = keep.tile([P, I], F32, name="ax")
-        mx = keep.tile([P, CHUNKS], F32, name="mx")
+        last_max = keep.tile([P, 1], F32, name="last_max")
+        chunk_max = [ax[:, j : j + 1] for j in range(LAST)] + [last_max[:]]
         px = keep.tile([P, I], F32, name="px")
+
         for j in range(CHUNKS):
-            cols = slice(j * N, (j + 1) * N)
-            bank = psum.tile([P, N], F32, name=f"bank{j}", tag=f"bank{j}")
+            scores = psum.tile([P, N], F32, name=f"scores{j}", tag=f"bank{j}")
             nc.tensor.matmul_mx(
-                out=bank[:],
+                out=scores[:],
                 lhsT=hid_codes[:].bitcast(FP8X4),
-                lhsT_scale=hid_plane[:],
+                lhsT_scale=hid_scale_sb[:],
                 rhs=words[j].bitcast(FP4X4),
-                rhs_scale=voc_plane[:, cols],
+                rhs_scale=voc_scale_sb[:, chunk(j)],
                 start=True,
                 stop=True,
             )
             nc.vector.tensor_scalar(
-                out=a_sb[:, cols], in0=bank[:], scalar1=1.0, scalar2=None, op0=ALU.mult, op1=ALU.max,
-                accum_out=mx[:, j : j + 1],
+                out=a_sb[:, chunk(j)], in0=scores[:], scalar1=1.0, scalar2=None, op0=ALU.mult, op1=ALU.max,
+                accum_out=chunk_max[j],
             )
             if j == 0:
                 nc.gpsimd.tensor_scalar(
-                    out=ns[:, 0:1], in0=mx[:, 0:1], scalar1=-1.0, scalar2=0.0, op0=ALU.mult, op1=ALU.add
+                    out=neg_run[:, 0:1], in0=chunk_max[0], scalar1=-1.0, scalar2=0.0,
+                    op0=ALU.mult, op1=ALU.add,
                 )
-            elif j < CHUNKS - 1:
+            elif j < LAST:
                 nc.gpsimd.tensor_scalar(
-                    out=ns[:, j : j + 1], in0=mx[:, j : j + 1], scalar1=-1.0, scalar2=ns[:, j - 1 : j],
-                    op0=ALU.mult, op1=ALU.min,
+                    out=neg_run[:, j : j + 1], in0=chunk_max[j], scalar1=-1.0,
+                    scalar2=neg_run[:, j - 1 : j], op0=ALU.mult, op1=ALU.min,
                 )
 
-        def exp_chunk(j):
-            cols = slice(j * N, (j + 1) * N)
-            shift = ns[:, j : j + 1] if j < CHUNKS - 1 else nm[:]
+        def exp_chunk(j, neg_shift):
             nc.scalar.activation(
-                out=p_sb[:, cols], in_=a_sb[:, cols], func=ACT.Exp, bias=shift, accum_out=zs[:, j : j + 1]
+                out=p_sb[:, chunk(j)], in_=a_sb[:, chunk(j)], func=ACT.Exp, bias=neg_shift,
+                accum_out=z_parts[:, j : j + 1],
             )
 
-        for j in range(CHUNKS - 1):
-            exp_chunk(j)
-        last = CHUNKS - 1
-        nc.gpsimd.tensor_scalar(
-            out=nm[:], in0=mx[:, last:], scalar1=-1.0, scalar2=ns[:, last - 1 :], op0=ALU.mult, op1=ALU.min
+        for j in range(LAST):
+            exp_chunk(j, neg_run[:, j : j + 1])
+        nc.vector.tensor_scalar(
+            out=neg_max[:], in0=chunk_max[LAST], scalar1=-1.0, scalar2=neg_run[:, LAST - 1 :],
+            op0=ALU.mult, op1=ALU.min,
         )
         nc.vector.tensor_copy(out=ax[:], in_=a_sb[:].indirect(offsets[:]))
-        exp_chunk(last)
-        nc.scalar.activation(out=f[:, :last], in_=ns[:], func=ACT.Exp, scale=-1.0, bias=nm[:])
-        nc.scalar.activation(out=px[:], in_=ax[:], func=ACT.Exp, bias=nm[:])
+        exp_chunk(LAST, neg_max[:])
+        nc.scalar.activation(out=mend[:, :LAST], in_=neg_run[:], func=ACT.Exp, scale=-1.0, bias=neg_max[:])
+        nc.scalar.activation(out=px[:], in_=ax[:], func=ACT.Exp, bias=neg_max[:])
         sq = keep.tile([P, I + 1 + CHUNKS], F32, name="sq")
         nc.scalar.activation(out=sq[:, :I], in_=px[:], func=ACT.Square)
 
@@ -143,10 +171,7 @@ def tile_attend_bcoverage_heads_kernel(tc, hid, voc_words, voc_scales, aim, cw1,
         cw_all = spread(cw_rows, "cw")
         sw_all = spread(sw_rows, "sw")
 
-        def by4(t):
-            return t[:].rearrange("p (n c) -> p n c", c=PACK)
-
-        def col(name):
+        def column(name):
             return keep.tile([P, 1], F32, name=name)
 
         w = keep.tile([P, I], F32, name="w")
@@ -154,86 +179,82 @@ def tile_attend_bcoverage_heads_kernel(tc, hid, voc_words, voc_scales, aim, cw1,
         y = keep.tile([P, I], F32, name="y")
         sw_sb = keep.tile([P, I + 1], F32, name="sw_sb")
         pm = sw_sb[:, I:]
-        z, rpm, rz, big_a, acc, nrpm = [col(n) for n in ("z", "rpm", "rz", "big_a", "acc", "nrpm")]
-        fz = keep.tile([P, CHUNKS], F32, name="fz")
+        z, rpm, rz, x_scale, x_sum, neg_rpm = [
+            column(name) for name in ("z", "rpm", "rz", "x_scale", "x_sum", "neg_rpm")
+        ]
+        z_mended = keep.tile([P, CHUNKS], F32, name="z_mended")
         factors = keep.tile([P, 2], F32, name="factors")
         aims = keep.tile([P, 2], F32, name="aims")
-        rzs = keep.tile([P, 2], F32, name="rzs")
-        terms = keep.tile([P, CHUNKS + 2], F32, name="terms")
+        rz_scaled = keep.tile([P, 2], F32, name="rz_scaled")
+        terms = keep.tile([P, 2 + CHUNKS], F32, name="terms")
         nc.vector.memset(factors[:, 0:1], -2048.0)
         nc.vector.memset(factors[:, 1:2], 1.0 / 512.0)
         nc.vector.memset(aims[:, 1:2], 0.0)
         nc.vector.tensor_scalar(out=aims[:, 0:1], in0=aim_col[:], scalar1=2048.0, scalar2=None, op0=ALU.mult)
-        nc.vector.tensor_copy(out=sw_sb[:, :I].rearrange("p (n c) -> p n c", c=PACK), in_=sw_all)
+        nc.vector.tensor_copy(out=by_fours(sw_sb[:, :I]), in_=sw_all)
         nc.vector.scalar_tensor_tensor(
-            out=fz[:], in0=f[:], scalar=1.0, in1=zs[:], op0=ALU.mult, op1=ALU.mult, accum_out=z[:]
+            out=z_mended[:], in0=mend[:], scalar=1.0, in1=z_parts[:], op0=ALU.mult, op1=ALU.mult, accum_out=z[:]
         )
         nc.vector.reciprocal(out=rz[:], in_=z[:])
-        nc.vector.tensor_scalar(out=rzs[:], in0=factors[:], scalar1=rz[:], scalar2=None, op0=ALU.mult)
+        nc.vector.tensor_scalar(out=rz_scaled[:], in0=factors[:], scalar1=rz[:], scalar2=None, op0=ALU.mult)
         nc.vector.tensor_scalar(
-            out=terms[:, 2:], in0=f[:], scalar1=rz[:], scalar2=rz[:], op0=ALU.mult, op1=ALU.mult
+            out=terms[:, 2:], in0=mend[:], scalar1=rz[:], scalar2=rz[:], op0=ALU.mult, op1=ALU.mult
         )
         nc.vector.scalar_tensor_tensor(
-            out=by4(w), in0=by4(px), scalar=1.0, in1=cw_all, op0=ALU.mult, op1=ALU.mult, accum_out=pm
+            out=by_fours(w[:]), in0=by_fours(px[:]), scalar=1.0, in1=cw_all, op0=ALU.mult, op1=ALU.mult,
+            accum_out=pm,
         )
         nc.vector.reciprocal(out=rpm[:], in_=pm)
         nc.vector.scalar_tensor_tensor(
-            out=terms[:, :2], in0=rzs[:], scalar=pm, in1=aims[:], op0=ALU.mult, op1=ALU.add
+            out=terms[:, :2], in0=rz_scaled[:], scalar=pm, in1=aims[:], op0=ALU.mult, op1=ALU.add
         )
-        nc.vector.tensor_scalar(out=big_a[:], in0=rpm[:], scalar1=rpm[:], scalar2=512.0, op0=ALU.mult, op1=ALU.mult)
+        nc.vector.tensor_scalar(
+            out=x_scale[:], in0=rpm[:], scalar1=rpm[:], scalar2=512.0, op0=ALU.mult, op1=ALU.mult
+        )
         nc.vector.tensor_scalar(
             out=sq[:, I:], in0=terms[:, 1:], scalar1=terms[:, 0:1], scalar2=pm, op0=ALU.mult, op1=ALU.mult
         )
-        cj = sq[:, I + 1 :]
-        nc.vector.tensor_scalar(out=nrpm[:], in0=rpm[:], scalar1=-1.0, scalar2=None, op0=ALU.mult)
+        dz_chunk = sq[:, I + 1 :]
+        nc.vector.tensor_scalar(out=neg_rpm[:], in0=rpm[:], scalar1=-1.0, scalar2=None, op0=ALU.mult)
         nc.vector.scalar_tensor_tensor(
-            out=x[:], in0=sq[:, : I + 1], scalar=big_a[:], in1=sw_sb[:], op0=ALU.mult, op1=ALU.mult, accum_out=acc[:]
+            out=x[:], in0=sq[:, : I + 1], scalar=x_scale[:], in1=sw_sb[:], op0=ALU.mult, op1=ALU.mult,
+            accum_out=x_sum[:],
         )
-        nc.vector.tensor_scalar(out=y[:], in0=w[:], scalar1=acc[:], scalar2=nrpm[:], op0=ALU.mult, op1=ALU.mult)
+        nc.vector.tensor_scalar(
+            out=y[:], in0=w[:], scalar1=x_sum[:], scalar2=neg_rpm[:], op0=ALU.mult, op1=ALU.mult
+        )
         nc.vector.tensor_tensor(out=s1[:].indirect(offsets[:]), in0=x[:, :I], in1=y[:], op=ALU.add)
 
-        cp = keep.tile([P, V], F32, name="cp")
+        dz_p = keep.tile([P, V], F32, name="dz_p")
         turned = keep.tile([P, V], F32, name="turned")
         res = keep.tile([P, V], F32, name="res")
-        blocks = N // P
-
-        def block(t, j, b):
-            return t[:, j * N + b * P : j * N + (b + 1) * P]
-
         sums = []
         for j in range(CHUNKS):
             bank = psum.tile([P, N], F32, name=f"sum{j}", tag=f"bank{j}")
-            for b in range(blocks):
+            for b in range(BLOCKS):
                 nc.tensor.matmul(
                     out=block(bank, 0, b), lhsT=block(old_sb, j, b), rhs=ident[:], is_transpose=True,
                     start=(b == 0), stop=False,
                 )
             sums.append(bank)
-
-        def scale_and_add(j):
-            cols = slice(j * N, (j + 1) * N)
-            nc.scalar.activation(out=cp[:, cols], in_=p_sb[:, cols], func=ACT.Copy, scale=cj[:, j : j + 1])
-            for b in range(blocks):
+        for j in range(CHUNKS):
+            nc.scalar.activation(
+                out=dz_p[:, chunk(j)], in_=p_sb[:, chunk(j)], func=ACT.Copy, scale=dz_chunk[:, j : j + 1]
+            )
+            for b in range(BLOCKS):
                 nc.tensor.matmul(
-                    out=block(sums[j], 0, b), lhsT=block(cp, j, b), rhs=ident[:], is_transpose=True,
-                    start=False, stop=(b == blocks - 1),
+                    out=block(sums[j], 0, b), lhsT=block(dz_p, j, b), rhs=ident[:], is_transpose=True,
+                    start=False, stop=(b == BLOCKS - 1),
                 )
-
         backs = []
-
-        def turn_back(j):
-            cols = slice(j * N, (j + 1) * N)
-            nc.scalar.copy(out=turned[:, cols], in_=sums[j][:])
-            bank = psum.tile([P, N], F32, name=f"back{j}", tag=("back0", "back1", "sw", "cw")[j])
-            for b in range(blocks):
+        for j, tag in enumerate(("back0", "back1", "sw", "cw")):
+            nc.scalar.copy(out=turned[:, chunk(j)], in_=sums[j][:])
+            bank = psum.tile([P, N], F32, name=f"back{j}", tag=tag)
+            for b in range(BLOCKS):
                 nc.tensor.transpose(block(bank, 0, b), block(turned, j, b), ident[:])
             backs.append(bank)
 
-        for j in range(CHUNKS):
-            scale_and_add(j)
-        for j in range(CHUNKS):
-            turn_back(j)
-        for j, a, b in ((0, 0, 128), (0, 128, 512), (1, 0, 512), (2, 0, 512), (3, 0, 256), (3, 256, 384), (3, 384, 512)):
+        for j, a, b in PIECES:
             cols = slice(j * N + a, j * N + b)
             nc.vector.tensor_tensor(out=res[:, cols], in0=backs[j][:, a:b], in1=s1[:, cols], op=ALU.add)
             nc.sync.dma_start(out=out[:, cols], in_=res[:, cols])

from contextlib import ExitStack

import concourse.mybir as mybir
from concourse.masks import make_identity

D, V, Q, I = 512, 2048, 128, 512
FLOPS = 2 * D * V * Q

F32 = mybir.dt.float32
BF16 = mybir.dt.bfloat16
I32 = mybir.dt.int32
U32 = mybir.dt.uint32
U16 = mybir.dt.uint16
U8 = mybir.dt.uint8
FP8X4 = mybir.dt.float8_e4m3fn_x4
FP4X4 = mybir.dt.float4_e2m1fn_x4
ALU = mybir.AluOpType
ACT = mybir.ActivationFunctionType

P = 128
PACK = 4
N = 512
CHUNKS = V // N
LAST = CHUNKS - 1
BLOCKS = N // P
WORD_BYTES = 2
QUADRANT = 32
WORD_LOADS = ((0, 1), (1, 2), (2, 4))
PIECES = ((0, 0, 128), (0, 128, 512), (1, 0, 512), (2, 0, 512), (3, 0, 256), (3, 256, 384), (3, 384, 512))


def chunk(j):
    return slice(j * N, (j + 1) * N)


def block(tile, j, b):
    return tile[:, j * N + b * P : j * N + (b + 1) * P]


def by_fours(ap):
    return ap.rearrange("p (n c) -> p n c", c=PACK)


def tile_attend_bcoverage_heads_kernel(tc, hid, voc_words, voc_scales, aim, cw1, sw, old, offs, out):
    nc = tc.nc
    with ExitStack() as ctx:
        keep = ctx.enter_context(tc.tile_pool(name="keep", bufs=1))
        psum = ctx.enter_context(tc.psum_pool(name="psum", bufs=1))

        offsets = keep.tile([P, I // 16], U16, name="offsets")
        hid_raw = keep.tile([P, PACK, Q], F32, name="hid_raw")
        word_tiles = [
            keep.tile([P, (b - a) * WORD_BYTES * N], U8, name=f"words{a}", align_bytes=64) for a, b in WORD_LOADS
        ]
        words = [
            tile[:, (j - a) * WORD_BYTES * N : (j - a + 1) * WORD_BYTES * N]
            for tile, (a, b) in zip(word_tiles, WORD_LOADS)
            for j in range(a, b)
        ]
        voc_scale_sb = keep.tile([P, V], U8, name="voc_scale_sb", align_bytes=64)
        cw_rows = keep.tile([P, PACK], F32, name="cw_rows")
        sw_rows = keep.tile([P, PACK], F32, name="sw_rows")
        aim_col = keep.tile([P, 1], F32, name="aim_col")
        old_sb = keep.tile([P, V], F32, name="old_sb")
        s1 = keep.tile([P, V], F32, name="s1")
        ident = keep.tile([P, P], F32, name="ident")
        warm = keep.tile([P, 1], F32, name="warm")

        nc.sync.dma_start(out=hid_raw[:], in_=hid.rearrange("(p t) q -> p t q", t=PACK))
        for r in range(4):
            nc.sync.dma_start(
                out=voc_scale_sb[r:P:QUADRANT, :].bitcast(I32), in_=voc_scales[0, r:16:4, :].bitcast(I32)
            )
        for tile, (a, b) in zip(word_tiles, WORD_LOADS):
            nc.sync.dma_start(
                out=tile[:].bitcast(I32),
                in_=voc_words[0, :, a * WORD_BYTES * N : b * WORD_BYTES * N].bitcast(I32),
            )
        nc.sync.dma_start(offsets[:], offs)
        nc.sync.dma_start(out=cw_rows[:], in_=cw1.rearrange("o (p c) -> (o p) c", c=PACK))
        nc.sync.dma_start(out=sw_rows[:], in_=sw.rearrange("o (p c) -> (o p) c", c=PACK))
        nc.sync.dma_start(out=aim_col[:], in_=aim)
        for h in range(2):
            cols = slice(h * V // 2, (h + 1) * V // 2)
            nc.sync.dma_start(out=old_sb[:, cols], in_=old[:, cols])

        nc.vector.memset(warm[:], 0.0)
        nc.scalar.activation(out=warm[:], in_=warm[:], func=ACT.Exp)
        nc.vector.memset(s1[:], 0.0)
        make_identity(nc, ident[:])

        grouped = keep.tile([P, Q, PACK], BF16, name="grouped", align_bytes=64)
        hid_codes = keep.tile([P, Q], U32, name="hid_codes", align_bytes=64)
        hid_scale_sb = keep.tile([P, Q], U8, name="hid_scale_sb", align_bytes=64)
        halves = (slice(0, Q // 2), slice(Q // 2, Q))
        for qs, copy in zip(halves, (nc.vector.tensor_copy, nc.scalar.copy)):
            copy(
                out=grouped[:, qs, :].rearrange("p (c i) t -> p c t i", i=4),
                in_=hid_raw[:, :, qs].rearrange("p t (c i) -> p c t i", i=4),
            )
        for qs in halves:
            nc.vector.quantize_mx(
                out=hid_codes[:, qs].bitcast(FP8X4),
                scales=hid_scale_sb[:, qs],
                in_=grouped[:, qs, :].rearrange("p q t -> p (q t)"),
            )

        a_sb = keep.tile([P, V], F32, name="a_sb")
        p_sb = keep.tile([P, V], F32, name="p_sb")
        z_parts = keep.tile([P, CHUNKS], F32, name="z_parts")
        neg_run = keep.tile([P, LAST], F32, name="neg_run")
        neg_max = keep.tile([P, 1], F32, name="neg_max")
        mend = keep.tile([P, CHUNKS], F32, name="mend")
        nc.vector.memset(mend[:, LAST:], 1.0)
        ax = keep.tile([P, I], F32, name="ax")
        last_max = keep.tile([P, 1], F32, name="last_max")
        chunk_max = [ax[:, j : j + 1] for j in range(LAST)] + [last_max[:]]
        px = keep.tile([P, I], F32, name="px")

        for j in range(CHUNKS):
            scores = psum.tile([P, N], F32, name=f"scores{j}", tag=f"bank{j}")
            nc.tensor.matmul_mx(
                out=scores[:],
                lhsT=hid_codes[:].bitcast(FP8X4),
                lhsT_scale=hid_scale_sb[:],
                rhs=words[j].bitcast(FP4X4),
                rhs_scale=voc_scale_sb[:, chunk(j)],
                start=True,
                stop=True,
            )
            nc.vector.tensor_scalar(
                out=a_sb[:, chunk(j)], in0=scores[:], scalar1=1.0, scalar2=None, op0=ALU.mult, op1=ALU.max,
                accum_out=chunk_max[j],
            )
            if j == 0:
                nc.gpsimd.tensor_scalar(
                    out=neg_run[:, 0:1], in0=chunk_max[0], scalar1=-1.0, scalar2=0.0,
                    op0=ALU.mult, op1=ALU.add,
                )
            elif j < LAST:
                nc.gpsimd.tensor_scalar(
                    out=neg_run[:, j : j + 1], in0=chunk_max[j], scalar1=-1.0,
                    scalar2=neg_run[:, j - 1 : j], op0=ALU.mult, op1=ALU.min,
                )

        def exp_chunk(j, neg_shift):
            nc.scalar.activation(
                out=p_sb[:, chunk(j)], in_=a_sb[:, chunk(j)], func=ACT.Exp, bias=neg_shift,
                accum_out=z_parts[:, j : j + 1],
            )

        for j in range(LAST):
            exp_chunk(j, neg_run[:, j : j + 1])
        nc.vector.tensor_scalar(
            out=neg_max[:], in0=chunk_max[LAST], scalar1=-1.0, scalar2=neg_run[:, LAST - 1 :],
            op0=ALU.mult, op1=ALU.min,
        )
        nc.vector.tensor_copy(out=ax[:], in_=a_sb[:].indirect(offsets[:]))
        exp_chunk(LAST, neg_max[:])
        nc.scalar.activation(out=mend[:, :LAST], in_=neg_run[:], func=ACT.Exp, scale=-1.0, bias=neg_max[:])
        nc.scalar.activation(out=px[:], in_=ax[:], func=ACT.Exp, bias=neg_max[:])
        sq = keep.tile([P, I + 1 + CHUNKS], F32, name="sq")
        nc.scalar.activation(out=sq[:, :I], in_=px[:], func=ACT.Square)

        def spread(rows, tag):
            bank = psum.tile([P, PACK, P], F32, name="spread_" + tag, tag=tag)
            for c in range(PACK):
                nc.tensor.transpose(bank[:, c, :], rows[:, c : c + 1].to_broadcast([P, P]), ident[:])
            return bank[:].rearrange("p c n -> p n c")

        cw_all = spread(cw_rows, "cw")
        sw_all = spread(sw_rows, "sw")

        def column(name):
            return keep.tile([P, 1], F32, name=name)

        w = keep.tile([P, I], F32, name="w")
        x = keep.tile([P, I + 1], F32, name="x")
        y = keep.tile([P, I], F32, name="y")
        sw_sb = keep.tile([P, I + 1], F32, name="sw_sb")
        pm = sw_sb[:, I:]
        z, rpm, rz, x_scale, x_sum, neg_rpm = [
            column(name) for name in ("z", "rpm", "rz", "x_scale", "x_sum", "neg_rpm")
        ]
        z_mended = keep.tile([P, CHUNKS], F32, name="z_mended")
        factors = keep.tile([P, 2], F32, name="factors")
        aims = keep.tile([P, 2], F32, name="aims")
        rz_scaled = keep.tile([P, 2], F32, name="rz_scaled")
        terms = keep.tile([P, 2 + CHUNKS], F32, name="terms")
        nc.vector.memset(factors[:, 0:1], -2048.0)
        nc.vector.memset(factors[:, 1:2], 1.0 / 512.0)
        nc.vector.memset(aims[:, 1:2], 0.0)
        nc.vector.tensor_scalar(out=aims[:, 0:1], in0=aim_col[:], scalar1=2048.0, scalar2=None, op0=ALU.mult)
        nc.vector.tensor_copy(out=by_fours(sw_sb[:, :I]), in_=sw_all)
        nc.vector.scalar_tensor_tensor(
            out=z_mended[:], in0=mend[:], scalar=1.0, in1=z_parts[:], op0=ALU.mult, op1=ALU.mult, accum_out=z[:]
        )
        nc.vector.reciprocal(out=rz[:], in_=z[:])
        nc.vector.tensor_scalar(out=rz_scaled[:], in0=factors[:], scalar1=rz[:], scalar2=None, op0=ALU.mult)
        nc.vector.tensor_scalar(
            out=terms[:, 2:], in0=mend[:], scalar1=rz[:], scalar2=rz[:], op0=ALU.mult, op1=ALU.mult
        )
        nc.vector.scalar_tensor_tensor(
            out=by_fours(w[:]), in0=by_fours(px[:]), scalar=1.0, in1=cw_all, op0=ALU.mult, op1=ALU.mult,
            accum_out=pm,
        )
        nc.vector.reciprocal(out=rpm[:], in_=pm)
        nc.vector.scalar_tensor_tensor(
            out=terms[:, :2], in0=rz_scaled[:], scalar=pm, in1=aims[:], op0=ALU.mult, op1=ALU.add
        )
        nc.vector.tensor_scalar(
            out=x_scale[:], in0=rpm[:], scalar1=rpm[:], scalar2=512.0, op0=ALU.mult, op1=ALU.mult
        )
        nc.vector.tensor_scalar(
            out=sq[:, I:], in0=terms[:, 1:], scalar1=terms[:, 0:1], scalar2=pm, op0=ALU.mult, op1=ALU.mult
        )
        dz_chunk = sq[:, I + 1 :]
        nc.vector.tensor_scalar(out=neg_rpm[:], in0=rpm[:], scalar1=-1.0, scalar2=None, op0=ALU.mult)
        nc.vector.scalar_tensor_tensor(
            out=x[:], in0=sq[:, : I + 1], scalar=x_scale[:], in1=sw_sb[:], op0=ALU.mult, op1=ALU.mult,
            accum_out=x_sum[:],
        )
        nc.vector.tensor_scalar(
            out=y[:], in0=w[:], scalar1=x_sum[:], scalar2=neg_rpm[:], op0=ALU.mult, op1=ALU.mult
        )
        nc.vector.tensor_tensor(out=s1[:].indirect(offsets[:]), in0=x[:, :I], in1=y[:], op=ALU.add)

        dz_p = keep.tile([P, V], F32, name="dz_p")
        turned = keep.tile([P, V], F32, name="turned")
        res = keep.tile([P, V], F32, name="res")
        sums = []
        for j in range(CHUNKS):
            bank = psum.tile([P, N], F32, name=f"sum{j}", tag=f"bank{j}")
            for b in range(BLOCKS):
                nc.tensor.matmul(
                    out=block(bank, 0, b), lhsT=block(old_sb, j, b), rhs=ident[:], is_transpose=True,
                    start=(b == 0), stop=False,
                )
            sums.append(bank)
        for j in range(CHUNKS):
            nc.scalar.activation(
                out=dz_p[:, chunk(j)], in_=p_sb[:, chunk(j)], func=ACT.Copy, scale=dz_chunk[:, j : j + 1]
            )
            for b in range(BLOCKS):
                nc.tensor.matmul(
                    out=block(sums[j], 0, b), lhsT=block(dz_p, j, b), rhs=ident[:], is_transpose=True,
                    start=False, stop=(b == BLOCKS - 1),
                )
        backs = []
        for j, tag in enumerate(("back0", "back1", "sw", "cw")):
            nc.scalar.copy(out=turned[:, chunk(j)], in_=sums[j][:])
            bank = psum.tile([P, N], F32, name=f"back{j}", tag=tag)
            for b in range(BLOCKS):
                nc.tensor.transpose(block(bank, 0, b), block(turned, j, b), ident[:])
            backs.append(bank)

        for j, a, b in PIECES:
            cols = slice(j * N + a, j * N + b)
            nc.vector.tensor_tensor(out=res[:, cols], in0=backs[j][:, a:b], in1=s1[:, cols], op=ALU.add)
            nc.sync.dma_start(out=out[:, cols], in_=res[:, cols])
